import numpy as np
CORES = [5,13,21,29,37,45,53,61,69,77,85,93,101,109,117,125]
N = 16
def setup_inputs(rng):
    return {"x1": rng.standard_normal((N, 128, 16), dtype=np.float32), "x2": rng.standard_normal((N, 128, 256), dtype=np.float32)}
def reference(x1, x2):
    out = []
    s = x1.sum(axis=0, dtype=np.float64).astype(x1.dtype)
    out.append(np.broadcast_to(s, (N,) + s.shape))
    b = 256 // N
    bl = x2.reshape(N, 128, N, b)
    out.append(np.ascontiguousarray(bl.transpose(2, 1, 0, 3)).reshape(N, 128, 256))
    return {"y1": out[0], "y2": out[1]}

@@ -1,0 +1,101 @@
+from concourse.bass import DstId, RemoteDMATransfer
+
+B = 16
+NPIECE = 8
+FWD_FAR = 2
+ADDER = 3
+FWD_MATE = 6
+
+SCRATCH = {
+    "sbx2": ("sbuf", [128, 256], "float32"),
+    "land": ("sbuf", [128, 256], "float32"),
+    "x1d": ("dram", [NPIECE, 128, 2], "float32"),
+    "gath": ("dram", [NPIECE, 128, 2], "float32"),
+    "part": ("dram", [128, 2], "float32"),
+    "res": ("dram", [NPIECE, 128, 2], "float32"),
+}
+SEMAPHORES = ["ld1", "ld2", "own", "sent", "hand", "arr", "gath", "part", "res", "st"]
+
+
+def blk(j):
+    return slice(j * B, (j + 1) * B)
+
+
+def dst_id(topo, c):
+    rid, pid, _se = topo.addr(c)
+    return DstId(rid=rid, pnc=pid)
+
+
+def rank_program(g, core, T, topo):
+    chip, k = divmod(core, 8)
+    par = chip & 1
+    n = len(T.cores)
+    rank_core = T.cores[chip]
+    r = chip
+    same = [j for j in range(n) if j != r and (j & 1) == par]
+    far = [j for j in range(n) if (j & 1) != par and j != (r ^ 1)]
+    mate = r ^ 1
+
+    if core == rank_core:
+        g.scalar.dma_start(T.x1d[:], T.x1[:, :]).then_inc(T.sem.ld1, 16)
+        g.sync.dma_start(T.sbx2[:, :], T.x2[:, :]).then_inc(T.sem.ld2, 16)
+        g.scalar.dma_start(T.land[:, blk(r)], T.x2[:, blk(r)]).then_inc(T.sem.own, 16)
+
+        g.wait_ge(T.sem.ld1, 16)
+        g.remote_dma_fused(
+            [RemoteDMATransfer(dst_ids=[dst_id(topo, (2 * q + par) * 8 + ADDER)], dma_engine_mask=1 << q,
+                               remote_sem=T.sem.gath, src=T.x1d[q], dst=T.gath[r // 2])
+             for q in range(NPIECE)],
+            local_sem=T.sem.sent)
+
+        g.wait_ge(T.sem.ld2, 16)
+        tr = []
+        for e, j in enumerate(same):
+            tr.append(RemoteDMATransfer(dst_ids=[dst_id(topo, T.cores[j])], dma_engine_mask=1 << e,
+                                        remote_sem=T.sem.arr, src=T.sbx2[:, blk(j)], dst=T.land[:, blk(r)]))
+        tr.append(RemoteDMATransfer(dst_ids=[dst_id(topo, chip * 8 + FWD_MATE)], dma_engine_mask=1 << 7,
+                                    remote_sem=T.sem.hand, src=T.sbx2[:, blk(mate)], dst=T.sbx2[:, blk(mate)]))
+        for e, j in enumerate(far):
+            tr.append(RemoteDMATransfer(dst_ids=[dst_id(topo, chip * 8 + FWD_FAR)], dma_engine_mask=1 << (8 + e),
+                                        remote_sem=T.sem.hand, src=T.sbx2[:, blk(j)], dst=T.sbx2[:, blk(j)]))
+        g.remote_dma_fused(tr, local_sem=T.sem.sent)
+
+        g.sync.wait_ge(T.sem.res, NPIECE)
+        g.sync.dma_start(T.y1[:, :], T.res[:]).then_inc(T.sem.st, 16)
+        g.scalar.wait_ge(T.sem.arr, 7 + 7 + 8)
+        g.scalar.wait_ge(T.sem.own, 16)
+        g.scalar.dma_start(T.y2[:, :], T.land[:, :]).then_inc(T.sem.st, 16)
+
+        g.wait_ge(T.sem.sent, NPIECE + 15)
+        g.wait_ge(T.sem.st, 32)
+
+    elif k == FWD_FAR:
+        g.wait_ge(T.sem.hand, 7)
+        g.remote_dma_fused(
+            [RemoteDMATransfer(dst_ids=[dst_id(topo, T.cores[j])], dma_engine_mask=1 << e,
+                               remote_sem=T.sem.arr, src=T.sbx2[:, blk(j)], dst=T.land[:, blk(r)])
+             for e, j in enumerate(far)],
+            local_sem=T.sem.sent)
+        g.wait_ge(T.sem.sent, 7)
+
+    elif k == FWD_MATE:
+        g.wait_ge(T.sem.hand, 1)
+        rid, pid, _se = topo.addr(T.cores[mate])
+        g.remote_dma(T.land[:, blk(r)], T.sbx2[:, blk(mate)], T.sem.arr, T.sem.sent, pid, rid, 0xFF)
+        g.wait_ge(T.sem.sent, 8)
+
+    elif k == ADDER:
+        mine = [T.gath[i] for i in range(NPIECE)]
+        g.wait_ge(T.sem.gath, NPIECE)
+        g.remote_dma_fused(
+            [RemoteDMATransfer(dst_ids=[dst_id(topo, (chip ^ 1) * 8 + ADDER)], dma_engine_mask=1,
+                               remote_sem=T.sem.part, srcs=mine, dsts=[T.part[:, :]], alu_op=1)],
+            local_sem=T.sem.sent)
+        g.wait_ge(T.sem.part, 1)
+        plane = [j for j in range(n) if (j & 1) == par]
+        g.remote_dma_fused(
+            [RemoteDMATransfer(dst_ids=[dst_id(topo, T.cores[j]) for j in plane], dma_engine_mask=1,
+                               remote_sem=T.sem.res, srcs=mine + [T.part[:, :]],
+                               dsts=[T.res[chip // 2] for _j in plane], alu_op=1)],
+            local_sem=T.sem.sent)
+        g.wait_ge(T.sem.sent, 2)

@@ -1,10 +1,10 @@
 from concourse.bass import DstId, RemoteDMATransfer
 
 B = 16
+QB = 4
 NPIECE = 8
-FWD_FAR = 2
 ADDER = 3
-FWD_MATE = 6
+FORWARDERS = ((6, 7, 2, 3), (2, 3, 6, 7))
 
 SCRATCH = {
     "sbx2": ("sbuf", [128, 256], "float32"),
@@ -14,7 +14,7 @@ SCRATCH = {
     "part": ("dram", [128, 2], "float32"),
     "res": ("dram", [NPIECE, 128, 2], "float32"),
 }
-SEMAPHORES = ["ld1", "ld2", "own", "sent", "hand", "arr", "gath", "part", "res", "st"]
+SEMAPHORES = ["ld1", "ld2", "sent", "hand", "arr", "gath", "part", "res", "st"]
 
 
 def blk(j):
@@ -30,16 +30,13 @@ def rank_program(g, core, T, topo):
     chip, k = divmod(core, 8)
     par = chip & 1
     n = len(T.cores)
-    rank_core = T.cores[chip]
     r = chip
-    same = [j for j in range(n) if j != r and (j & 1) == par]
-    far = [j for j in range(n) if (j & 1) != par and j != (r ^ 1)]
-    mate = r ^ 1
+    fwd = FORWARDERS[par]
+    nq = n // QB
 
-    if core == rank_core:
+    if core == T.cores[r]:
         g.scalar.dma_start(T.x1d[:], T.x1[:, :]).then_inc(T.sem.ld1, 16)
         g.sync.dma_start(T.sbx2[:, :], T.x2[:, :]).then_inc(T.sem.ld2, 16)
-        g.scalar.dma_start(T.land[:, blk(r)], T.x2[:, blk(r)]).then_inc(T.sem.own, 16)
 
         g.wait_ge(T.sem.ld1, 16)
         g.remote_dma_fused(
@@ -50,47 +47,45 @@ def rank_program(g, core, T, topo):
 
         g.wait_ge(T.sem.ld2, 16)
         tr = []
-        for e, j in enumerate(same):
-            tr.append(RemoteDMATransfer(dst_ids=[dst_id(topo, T.cores[j])], dma_engine_mask=1 << e,
-                                        remote_sem=T.sem.arr, src=T.sbx2[:, blk(j)], dst=T.land[:, blk(r)]))
-        tr.append(RemoteDMATransfer(dst_ids=[dst_id(topo, chip * 8 + FWD_MATE)], dma_engine_mask=1 << 7,
-                                    remote_sem=T.sem.hand, src=T.sbx2[:, blk(mate)], dst=T.sbx2[:, blk(mate)]))
-        for e, j in enumerate(far):
-            tr.append(RemoteDMATransfer(dst_ids=[dst_id(topo, chip * 8 + FWD_FAR)], dma_engine_mask=1 << (8 + e),
-                                        remote_sem=T.sem.hand, src=T.sbx2[:, blk(j)], dst=T.sbx2[:, blk(j)]))
+        for o in range(nq):
+            q = (r // QB + o) % nq
+            cols = slice(q * QB * B, (q + 1) * QB * B)
+            tr.append(RemoteDMATransfer(dst_ids=[dst_id(topo, chip * 8 + fwd[o])], dma_engine_mask=0xF << (4 * o),
+                                        remote_sem=T.sem.hand, src=T.sbx2[:, cols], dst=T.sbx2[:, cols]))
         g.remote_dma_fused(tr, local_sem=T.sem.sent)
 
         g.sync.wait_ge(T.sem.res, NPIECE)
         g.sync.dma_start(T.y1[:, :], T.res[:]).then_inc(T.sem.st, 16)
-        g.scalar.wait_ge(T.sem.arr, 7 + 7 + 8)
-        g.scalar.wait_ge(T.sem.own, 16)
+        g.scalar.wait_ge(T.sem.arr, 2 * n)
         g.scalar.dma_start(T.y2[:, :], T.land[:, :]).then_inc(T.sem.st, 16)
 
-        g.wait_ge(T.sem.sent, NPIECE + 15)
+        g.wait_ge(T.sem.sent, NPIECE + 16)
         g.wait_ge(T.sem.st, 32)
+        return
 
-    elif k == FWD_FAR:
-        g.wait_ge(T.sem.hand, 7)
-        g.remote_dma_fused(
-            [RemoteDMATransfer(dst_ids=[dst_id(topo, T.cores[j])], dma_engine_mask=1 << e,
-                               remote_sem=T.sem.arr, src=T.sbx2[:, blk(j)], dst=T.land[:, blk(r)])
-             for e, j in enumerate(far)],
-            local_sem=T.sem.sent)
-        g.wait_ge(T.sem.sent, 7)
+    if k not in fwd:
+        return
 
-    elif k == FWD_MATE:
-        g.wait_ge(T.sem.hand, 1)
-        rid, pid, _se = topo.addr(T.cores[mate])
-        g.remote_dma(T.land[:, blk(r)], T.sbx2[:, blk(mate)], T.sem.arr, T.sem.sent, pid, rid, 0xFF)
-        g.wait_ge(T.sem.sent, 8)
-
-    elif k == ADDER:
-        mine = [T.gath[i] for i in range(NPIECE)]
+    sent = 0
+    mine = [T.gath[i] for i in range(NPIECE)]
+    if k == ADDER:
         g.wait_ge(T.sem.gath, NPIECE)
         g.remote_dma_fused(
             [RemoteDMATransfer(dst_ids=[dst_id(topo, (chip ^ 1) * 8 + ADDER)], dma_engine_mask=1,
                                remote_sem=T.sem.part, srcs=mine, dsts=[T.part[:, :]], alu_op=1)],
             local_sem=T.sem.sent)
+        sent += 1
+
+    q = (r // QB + fwd.index(k)) % nq
+    g.wait_ge(T.sem.hand, 4)
+    g.remote_dma_fused(
+        [RemoteDMATransfer(dst_ids=[dst_id(topo, T.cores[j])], dma_engine_mask=0x3 << (2 * e),
+                           remote_sem=T.sem.arr, src=T.sbx2[:, blk(j)], dst=T.land[:, blk(r)])
+         for e, j in enumerate(range(q * QB, (q + 1) * QB))],
+        local_sem=T.sem.sent)
+    sent += 2 * QB
+
+    if k == ADDER:
         g.wait_ge(T.sem.part, 1)
         plane = [j for j in range(n) if (j & 1) == par]
         g.remote_dma_fused(
@@ -98,4 +93,5 @@ def rank_program(g, core, T, topo):
                                remote_sem=T.sem.res, srcs=mine + [T.part[:, :]],
                                dsts=[T.res[chip // 2] for _j in plane], alu_op=1)],
             local_sem=T.sem.sent)
-        g.wait_ge(T.sem.sent, 2)
+        sent += 1
+    g.wait_ge(T.sem.sent, sent)

from concourse.bass import DstId, RemoteDMATransfer

B = 16
QB = 4
NPIECE = 8
ADDER = 3
FORWARDERS = ((6, 7, 2, 3), (2, 3, 6, 7))

SCRATCH = {
    "sbx2": ("sbuf", [128, 256], "float32"),
    "land": ("sbuf", [128, 256], "float32"),
    "x1d": ("dram", [NPIECE, 128, 2], "float32"),
    "gath": ("dram", [NPIECE, 128, 2], "float32"),
    "part": ("dram", [128, 2], "float32"),
    "res": ("dram", [NPIECE, 128, 2], "float32"),
}
SEMAPHORES = ["ld1", "ld2", "sent", "hand", "arr", "gath", "part", "res", "st"]


def blk(j):
    return slice(j * B, (j + 1) * B)


def dst_id(topo, c):
    rid, pid, _se = topo.addr(c)
    return DstId(rid=rid, pnc=pid)


def rank_program(g, core, T, topo):
    chip, k = divmod(core, 8)
    par = chip & 1
    n = len(T.cores)
    r = chip
    fwd = FORWARDERS[par]
    nq = n // QB

    if core == T.cores[r]:
        g.scalar.dma_start(T.x1d[:], T.x1[:, :]).then_inc(T.sem.ld1, 16)
        g.sync.dma_start(T.sbx2[:, :], T.x2[:, :]).then_inc(T.sem.ld2, 16)

        g.wait_ge(T.sem.ld1, 16)
        g.remote_dma_fused(
            [RemoteDMATransfer(dst_ids=[dst_id(topo, (2 * q + par) * 8 + ADDER)], dma_engine_mask=1 << q,
                               remote_sem=T.sem.gath, src=T.x1d[q], dst=T.gath[r // 2])
             for q in range(NPIECE)],
            local_sem=T.sem.sent)

        g.wait_ge(T.sem.ld2, 16)
        tr = []
        for o in range(nq):
            q = (r // QB + o) % nq
            cols = slice(q * QB * B, (q + 1) * QB * B)
            tr.append(RemoteDMATransfer(dst_ids=[dst_id(topo, chip * 8 + fwd[o])], dma_engine_mask=0xF << (4 * o),
                                        remote_sem=T.sem.hand, src=T.sbx2[:, cols], dst=T.sbx2[:, cols]))
        g.remote_dma_fused(tr, local_sem=T.sem.sent)

        g.sync.wait_ge(T.sem.res, NPIECE)
        g.sync.dma_start(T.y1[:, :], T.res[:]).then_inc(T.sem.st, 16)
        g.scalar.wait_ge(T.sem.arr, 2 * n)
        g.scalar.dma_start(T.y2[:, :], T.land[:, :]).then_inc(T.sem.st, 16)

        g.wait_ge(T.sem.sent, NPIECE + 16)
        g.wait_ge(T.sem.st, 32)
        return

    if k not in fwd:
        return

    sent = 0
    mine = [T.gath[i] for i in range(NPIECE)]
    if k == ADDER:
        g.wait_ge(T.sem.gath, NPIECE)
        g.remote_dma_fused(
            [RemoteDMATransfer(dst_ids=[dst_id(topo, (chip ^ 1) * 8 + ADDER)], dma_engine_mask=1,
                               remote_sem=T.sem.part, srcs=mine, dsts=[T.part[:, :]], alu_op=1)],
            local_sem=T.sem.sent)
        sent += 1

    q = (r // QB + fwd.index(k)) % nq
    g.wait_ge(T.sem.hand, 4)
    g.remote_dma_fused(
        [RemoteDMATransfer(dst_ids=[dst_id(topo, T.cores[j])], dma_engine_mask=0x3 << (2 * e),
                           remote_sem=T.sem.arr, src=T.sbx2[:, blk(j)], dst=T.land[:, blk(r)])
         for e, j in enumerate(range(q * QB, (q + 1) * QB))],
        local_sem=T.sem.sent)
    sent += 2 * QB

    if k == ADDER:
        g.wait_ge(T.sem.part, 1)
        plane = [j for j in range(n) if (j & 1) == par]
        g.remote_dma_fused(
            [RemoteDMATransfer(dst_ids=[dst_id(topo, T.cores[j]) for j in plane], dma_engine_mask=1,
                               remote_sem=T.sem.res, srcs=mine + [T.part[:, :]],
                               dsts=[T.res[chip // 2] for _j in plane], alu_op=1)],
            local_sem=T.sem.sent)
        sent += 1
    g.wait_ge(T.sem.sent, sent)
